import numpy as np
import ml_dtypes


def mxq(x, axis, fmt="e4m3"):
    dtype, down = {"e4m3": (ml_dtypes.float8_e4m3fn, 7), "e5m2": (ml_dtypes.float8_e5m2, 14)}[fmt]
    v = np.moveaxis(np.asarray(x, np.float32).astype(ml_dtypes.bfloat16).astype(np.float64), axis, -1)
    blocks = v.reshape(v.shape[:-1] + (-1, 32))
    amax = np.abs(blocks).max(-1, keepdims=True)
    byte = np.maximum(np.where(amax > 0, np.frexp(amax)[1] - 1 + 127, 0) - down, 1)
    scale = np.exp2(byte - 127.0)
    codes = (blocks / scale).astype(np.float32).astype(dtype).astype(np.float64)
    return np.moveaxis((codes * scale).reshape(v.shape), -1, axis)


WIDE = False


def mx_kscale(k):
    if not WIDE:
        return np.ones(k)
    levels = np.array([30, -30])
    if k % 512:
        return np.exp2(np.random.permutation(np.resize(levels, k // 32))).repeat(32)
    a = np.empty((k // 512, 16))
    for p in range(k // 512):
        a[p, :8] = np.random.permutation(np.resize(levels, 8))
        for g in range(8):
            far = levels[np.abs(levels - a[p, g]) >= 10]
            a[p, g + 8] = far[np.random.randint(len(far))]
    return np.exp2(a.ravel()).repeat(32)


BF16 = ml_dtypes.bfloat16


def bf(x):
    return np.asarray(x, np.float32).astype(BF16)


def f64(x):
    return np.asarray(x).astype(np.float64)


E2M1 = np.array([0.0, 0.5, 1.0, 1.5, 2.0, 3.0, 4.0, 6.0, -0.0, -0.5, -1.0, -1.5, -2.0, -3.0, -4.0, -6.0])


def pack_weight(w, fmt):
    k, n = w.shape
    w = f64(bf(w)).reshape(k // 32, 32, n)
    amax = np.abs(w).max(1)
    if fmt in ("e4m3", "e5m2"):
        byte = np.frexp(amax)[1] - 1 + 127 - (7 if fmt == "e4m3" else 14)
    else:
        mant, ex = np.frexp(amax / 6.0)
        byte = np.where(mant > 0.5, ex, ex - 1) + 127
    byte = np.clip(np.where(amax > 0, byte, 1), 1, 254)
    scaled = (w * np.exp2(127.0 - byte)[:, None, :]).reshape(k, n).astype(np.float32)
    by_word = np.ascontiguousarray(scaled.reshape(k // 512, 128, 4, n).transpose(0, 1, 3, 2))
    if fmt in ("e4m3", "e5m2"):
        words = by_word.astype(ml_dtypes.float8_e4m3fn if fmt == "e4m3" else ml_dtypes.float8_e5m2).view(np.uint8)
    else:
        c = by_word.astype(ml_dtypes.float4_e2m1fn).view(np.uint8) & 0xF
        words = c[..., 0::2] | (c[..., 1::2] << 4)
    return np.ascontiguousarray(words), np.ascontiguousarray(byte.astype(np.uint8).reshape(k // 512, 16, n))


def unpack_weight(words, scales, fmt):
    g, p, n, _ = words.shape
    if fmt in ("e4m3", "e5m2"):
        vals = np.ascontiguousarray(words).view(ml_dtypes.float8_e4m3fn if fmt == "e4m3" else ml_dtypes.float8_e5m2).astype(np.float64)
    else:
        nib = np.empty((g, p, n, 4), np.uint8)
        nib[..., 0::2] = words & 0xF
        nib[..., 1::2] = words >> 4
        vals = E2M1[nib]
    vals = vals * np.repeat(np.exp2(scales.astype(np.float64) - 127.0), 8, axis=1)[..., None]
    return vals.transpose(0, 1, 3, 2).reshape(g * 512, n)


E, C, D, F = 4, 1024, 1024, 512
BETA = 0.9


def setup_inputs():
    s, t = mx_kscale(D), mx_kscale(C)
    G = np.random.standard_t(5, (D, E * C)) * s[:, None] * np.tile(t, E)
    g_words, g_scales = pack_weight(G, "e5m2")
    w2 = np.random.standard_normal((E, D, F)) / np.sqrt(D) / s[:, None]
    z = np.random.standard_normal((E, C, F))
    sg = 1.0 / (1.0 + np.exp(-z))
    d = sg * (1.0 + z * (1.0 - sg))
    gate = np.random.uniform(0.25, 1.0, (E, C))
    x = np.random.standard_normal((E, C, D)) / np.sqrt(C) / t[:, None]
    m = 0.5 * np.random.standard_normal((E, D, F))
    return {"g_words": g_words, "g_scales": g_scales, "w2": bf(w2), "d": bf(d),
            "gate": bf(gate), "x": bf(x), "m": bf(m)}


def reference(g_words, g_scales, w2, d, gate, x, m):
    g = unpack_weight(g_words, g_scales, "e5m2").T.reshape(E, C, D)
    da = g @ mxq(f64(w2), 1, "e4m3")
    dh = da * f64(gate)[:, :, None] * f64(d)
    dw = mxq(f64(x), 1, "e4m3").swapaxes(1, 2) @ mxq(dh, 1, "e5m2")
    return BETA * f64(m) + dw

@@ -1,0 +1,262 @@
+from contextlib import ExitStack
+
+import concourse.mybir as mybir
+
+E, C, D, F = 4, 1024, 1024, 512
+BETA = 0.9
+FLOPS = 2 * (2 * E * C * D * F)
+
+F32 = mybir.dt.float32
+BF16 = mybir.dt.bfloat16
+I32 = mybir.dt.int32
+U32 = mybir.dt.uint32
+U8 = mybir.dt.uint8
+E4M3 = mybir.dt.float8_e4m3fn_x4
+E5M2 = mybir.dt.float8_e5m2_x4
+MULT = mybir.AluOpType.mult
+ADD = mybir.AluOpType.add
+
+P = 128
+PACK = 4
+K_PASS = P * PACK
+HALVES = C // K_PASS
+
+VECTOR_COPIES = {("w", 0, 1), ("x", 0, 0, 1), ("x", 1, 1, 1), ("x", 2, 1, 1), ("dh", 3, 1)}
+GPSIMD_COPIES = set()
+
+
+def tile_expert_inner_weight_gradient_e3_kernel(tc, g_words, g_scales, w2, d, gate, x, m, out):
+    nc = tc.nc
+
+    with ExitStack() as ctx:
+        raw = ctx.enter_context(tc.tile_pool(name="raw", bufs=2))
+        work = ctx.enter_context(tc.tile_pool(name="work", bufs=2))
+        keep = ctx.enter_context(tc.tile_pool(name="keep", bufs=1))
+        psum = ctx.enter_context(tc.psum_pool(name="psum", bufs=8))
+
+        T = {}
+
+        def load_w(e, g):
+            t = raw.tile([P, PACK, F], BF16, name="w_raw", tag="w_raw", bufs=4)
+            nc.sync.dma_start(out=t[:], in_=w2[e, g * K_PASS:(g + 1) * K_PASS, :].rearrange("(p t) f -> p t f", t=PACK))
+            T["w_raw", e, g] = t
+
+        def load_g(e):
+            t = raw.tile([P, 2, C], I32, name="g_raw", tag="g_raw", bufs=2)
+            src = g_words.rearrange("g p n t -> p g (n t)")[:, :, 4 * C * e:4 * C * (e + 1)].bitcast(I32)
+            nc.sync.dma_start(out=t[:], in_=src)
+            T["g_raw", e] = t
+
+        def load_d(e):
+            t = raw.tile([P, HALVES, PACK, F], BF16, name="d_raw", tag="d_raw", bufs=2)
+            nc.sync.dma_start(out=t[:].rearrange("p h t f -> p h (t f)"), in_=d[e].rearrange("(h p t) f -> p h (t f)", h=HALVES, t=PACK))
+            T["d_raw", e] = t
+
+        def load_x(e, h):
+            t = raw.tile([P, PACK, D], BF16, name="x_raw", tag="x_raw", bufs=4)
+            nc.sync.dma_start(out=t[:], in_=x[e, h * K_PASS:(h + 1) * K_PASS, :].rearrange("(p t) f -> p t f", t=PACK))
+            T["x_raw", e, h] = t
+
+        def load_m(e):
+            t = raw.tile([P, 8, F], BF16, name="m_raw", tag="m_raw", bufs=2)
+            nc.sync.dma_start(out=t[:], in_=m[e].rearrange("(p r) f -> p r f", r=8))
+            T["m_raw", e] = t
+
+        def interleaving_copy(key, out, in_):
+            if key in VECTOR_COPIES:
+                nc.vector.tensor_copy(out=out, in_=in_)
+            elif key in GPSIMD_COPIES:
+                nc.gpsimd.tensor_scalar(out=out, in0=in_, scalar1=1.0, scalar2=0.0, op0=MULT, op1=ADD)
+            else:
+                nc.scalar.copy(out=out, in_=in_)
+
+        def interleave_w(e, g):
+            t = work.tile([P, F, PACK], BF16, name="w_grp", tag="w_grp", bufs=2, align_bytes=64)
+            interleaving_copy(
+                ("w", e, g),
+                out=t[:].rearrange("p (c i) t -> p c t i", i=4),
+                in_=T["w_raw", e, g][:].rearrange("p t (c i) -> p c t i", i=4),
+            )
+            T["w_grp", e, g] = t
+
+        def quantize_w(e, g):
+            codes = work.tile([P, F], U32, name="w_codes", tag="w_codes", bufs=4, align_bytes=64)
+            scales = work.tile([P, F], U8, name="w_scales", tag="w_scales", bufs=4, align_bytes=64)
+            nc.vector.quantize_mx(out=codes[:].bitcast(E4M3), scales=scales[:], in_=T["w_grp", e, g][:].rearrange("p c t -> p (c t)"))
+            T["w", e, g] = (codes, scales)
+
+        def permute_g(e):
+            codes = work.tile([P, 2, C], I32, name="g_codes", tag="g_codes", bufs=2, align_bytes=64)
+            nc.vector.tensor_copy(
+                out=codes[:].rearrange("p g (h t m) -> p (g h) m t", h=HALVES, t=PACK),
+                in_=T["g_raw", e][:].rearrange("p g (h m t) -> p (g h) m t", h=HALVES, t=PACK),
+            )
+            T["g_codes", e] = codes
+
+        def permute_gs(e):
+            scales = work.tile([P, 2, C], U8, name="g_scale", tag="g_scale", bufs=2, align_bytes=64)
+            for g in range(2):
+                nc.vector.tensor_copy(
+                    out=scales[:, g, :].rearrange("p (h t m) -> p h m t", h=HALVES, t=PACK),
+                    in_=gs_raw[:, g, C * e:C * (e + 1)].rearrange("p (h m t) -> p h m t", h=HALVES, t=PACK),
+                )
+            T["g_scale", e] = scales
+
+        def interleave_x(e, h, u):
+            if ("x_grp", e, h) not in T:
+                T["x_grp", e, h] = work.tile([P, D, PACK], BF16, name="x_grp", tag="x_grp", bufs=2, align_bytes=64)
+            interleaving_copy(
+                ("x", e, h, u),
+                out=T["x_grp", e, h][:].rearrange("p (u j m) t -> p u m t j", u=2, j=4)[:, u],
+                in_=T["x_raw", e, h][:].rearrange("p t (m u j) -> p u m t j", u=2, j=4)[:, u],
+            )
+
+        def quantize_x(e, h):
+            codes = work.tile([P, D], U32, name="x_codes", tag="x_codes", bufs=4, align_bytes=64)
+            scales = work.tile([P, D], U8, name="x_scales", tag="x_scales", bufs=4, align_bytes=64)
+            nc.vector.quantize_mx(out=codes[:].bitcast(E4M3), scales=scales[:], in_=T["x_grp", e, h][:].rearrange("p c t -> p (c t)"))
+            T["x", e, h] = (codes, scales)
+
+        def stage_1(e, h):
+            dh = work.tile([P, PACK, F], BF16, name="dh_lin", tag="dh_lin", bufs=2, align_bytes=64)
+            for t in range(PACK):
+                acc = psum.tile([P, F], F32, name="acc", tag="acc")
+                cols = slice((PACK * h + t) * P, (PACK * h + t + 1) * P)
+                for g in range(2):
+                    codes, scales = T["w", e, g]
+                    nc.tensor.matmul_mx(
+                        out=acc[:],
+                        lhsT=T["g_codes", e][:, g, cols].bitcast(E5M2),
+                        lhsT_scale=T["g_scale", e][:, g, cols],
+                        rhs=codes[:].bitcast(E4M3),
+                        rhs_scale=scales[:],
+                        start=(g == 0),
+                        stop=(g == 1),
+                    )
+                nc.vector.scalar_tensor_tensor(
+                    out=dh[:, t, :], in0=acc[:], scalar=gate_sb[:, HALVES * e + h, t:t + 1], in1=T["d_raw", e][:, h, t, :], op0=MULT, op1=MULT
+                )
+            T["dh_lin", e, h] = dh
+
+        def interleave_dh(e, h):
+            t = work.tile([P, F, PACK], BF16, name="dh_grp", tag="dh_grp", bufs=2, align_bytes=64)
+            interleaving_copy(
+                ("dh", e, h),
+                out=t[:].rearrange("p (c i) t -> p c t i", i=4),
+                in_=T["dh_lin", e, h][:].rearrange("p t (c i) -> p c t i", i=4),
+            )
+            T["dh_grp", e, h] = t
+
+        def quantize_dh(e, h):
+            codes = work.tile([P, F], U32, name="dh_codes", tag="dh_codes", bufs=4, align_bytes=64)
+            scales = work.tile([P, F], U8, name="dh_scales", tag="dh_scales", bufs=4, align_bytes=64)
+            nc.vector.quantize_mx(out=codes[:].bitcast(E5M2), scales=scales[:], in_=T["dh_grp", e, h][:].rearrange("p c t -> p (c t)"))
+            T["dh", e, h] = (codes, scales)
+
+        def stage_2(e, u):
+            o = work.tile([P, PACK, F], F32, name="o", tag="o", bufs=3)
+            T["o", e, u] = o
+            for j in range(PACK):
+                acc = psum.tile([P, F], F32, name="acc", tag="acc")
+                cols = slice((PACK * u + j) * P, (PACK * u + j + 1) * P)
+                for h in range(HALVES):
+                    xc, xs = T["x", e, h]
+                    hc, hs = T["dh", e, h]
+                    nc.tensor.matmul_mx(
+                        out=acc[:],
+                        lhsT=xc[:, cols].bitcast(E4M3),
+                        lhsT_scale=xs[:, cols],
+                        rhs=hc[:].bitcast(E5M2),
+                        rhs_scale=hs[:],
+                        start=(h == 0),
+                        stop=(h == HALVES - 1),
+                    )
+                nc.vector.scalar_tensor_tensor(out=o[:, j, :], in0=T["m_raw", e][:, PACK * u + j, :], scalar=BETA, in1=acc[:], op0=MULT, op1=ADD)
+                if e == E - 1 and (j % 2 == 1 or u == 1):
+                    j0 = j if u == 1 else j - 1
+                    store(e, u, j0, j + 1)
+
+        def store(e, u, j0=0, j1=PACK):
+            nc.sync.dma_start(out=out[e].rearrange("(p r) f -> p r f", r=8)[:, PACK * u + j0:PACK * u + j1, :], in_=T["o", e, u][:, j0:j1, :])
+
+        gs_raw = keep.tile([P, 2, E * C], U8, name="gs_raw", align_bytes=64)
+        nc.vector.memset(gs_raw[:].rearrange("p g n -> p (g n)").bitcast(I32), 0)
+        gate_sb = keep.tile([P, E * HALVES, PACK], BF16, name="gate_sb")
+        nc.scalar.dma_start(out=gate_sb[:], in_=gate.rearrange("e c -> (e c)").rearrange("(u p t) -> p u t", p=P, t=PACK))
+        load_w(0, 0)
+        load_w(0, 1)
+        for q in range(4):
+            nc.scalar.dma_start(
+                out=gs_raw[32 * q:32 * q + 4, :, :].bitcast(I32),
+                in_=g_scales[:, 4 * q:4 * q + 4, :].rearrange("g q n -> q g n").bitcast(I32),
+            )
+        load_x(0, 0)
+        load_g(0)
+        load_x(0, 1)
+        load_d(0)
+        load_w(1, 0)
+        load_w(1, 1)
+        load_g(1)
+        load_x(1, 0)
+        load_d(1)
+        load_m(0)
+        load_x(1, 1)
+        load_m(1)
+
+        interleave_w(0, 0)
+        interleave_w(0, 1)
+        interleave_x(0, 0, 0)
+        quantize_w(0, 0)
+        permute_g(0)
+        quantize_w(0, 1)
+        permute_gs(0)
+        interleave_x(0, 0, 1)
+
+        for e in range(E):
+            more = e + 1 < E
+            if not more:
+                interleave_x(e, 1, 0)
+            stage_1(e, 0)
+            interleave_dh(e, 0)
+            if more:
+                interleave_w(e + 1, 0)
+            else:
+                interleave_x(e, 1, 1)
+            quantize_x(e, 0)
+            stage_1(e, 1)
+            interleave_dh(e, 1)
+            if more:
+                interleave_w(e + 1, 1)
+            quantize_dh(e, 0)
+            if e > 0:
+                stage_2(e - 1, 0)
+            quantize_dh(e, 1)
+            if more:
+                permute_gs(e + 1)
+                permute_g(e + 1)
+                quantize_w(e + 1, 0)
+                interleave_x(e, 1, 0)
+                interleave_x(e, 1, 1)
+            if e > 0:
+                stage_2(e - 1, 1)
+            if more:
+                quantize_w(e + 1, 1)
+                interleave_x(e + 1, 0, 0)
+                interleave_x(e + 1, 0, 1)
+            quantize_x(e, 1)
+            if e + 2 < E:
+                load_w(e + 2, 0)
+                load_w(e + 2, 1)
+                load_g(e + 2)
+                load_x(e + 2, 0)
+                if e > 0:
+                    store(e - 1, 0)
+                    store(e - 1, 1)
+                load_d(e + 2)
+                load_x(e + 2, 1)
+                load_m(e + 2)
+            elif e > 0:
+                store(e - 1, 0)
+                store(e - 1, 1)
+        stage_2(E - 1, 0)
+        stage_2(E - 1, 1)

@@ -21,8 +21,8 @@ PACK = 4
 K_PASS = P * PACK
 HALVES = C // K_PASS
 
-VECTOR_COPIES = {("w", 0, 1), ("x", 0, 0, 1), ("x", 1, 1, 1), ("x", 2, 1, 1), ("dh", 3, 1)}
-GPSIMD_COPIES = set()
+VECTOR_COPIES = {("w", 0, 1), ("x", 0, 0, 1), ("x", 1, 1, 1), ("dh", 3, 1)}
+GPSIMD_W = (1, 2, 3)
 
 
 def tile_expert_inner_weight_gradient_e3_kernel(tc, g_words, g_scales, w2, d, gate, x, m, out):
@@ -65,18 +65,22 @@ def tile_expert_inner_weight_gradient_e3_kernel(tc, g_words, g_scales, w2, d, ga
         def interleaving_copy(key, out, in_):
             if key in VECTOR_COPIES:
                 nc.vector.tensor_copy(out=out, in_=in_)
-            elif key in GPSIMD_COPIES:
-                nc.gpsimd.tensor_scalar(out=out, in0=in_, scalar1=1.0, scalar2=0.0, op0=MULT, op1=ADD)
             else:
                 nc.scalar.copy(out=out, in_=in_)
 
         def interleave_w(e, g):
             t = work.tile([P, F, PACK], BF16, name="w_grp", tag="w_grp", bufs=2, align_bytes=64)
-            interleaving_copy(
-                ("w", e, g),
-                out=t[:].rearrange("p (c i) t -> p c t i", i=4),
-                in_=T["w_raw", e, g][:].rearrange("p t (c i) -> p c t i", i=4),
-            )
+            if e in GPSIMD_W:
+                for c in range(0, F, P):
+                    nc.gpsimd.tensor_scalar(
+                        out=t[:, c:c + P, :], in0=T["w_raw", e, g][:, :, c:c + P].rearrange("p t c -> p c t"), scalar1=1.0, scalar2=0.0, op0=MULT, op1=ADD
+                    )
+            else:
+                interleaving_copy(
+                    ("w", e, g),
+                    out=t[:].rearrange("p (c i) t -> p c t i", i=4),
+                    in_=T["w_raw", e, g][:].rearrange("p t (c i) -> p c t i", i=4),
+                )
             T["w_grp", e, g] = t
 
         def quantize_w(e, g):
@@ -154,7 +158,7 @@ def tile_expert_inner_weight_gradient_e3_kernel(tc, g_words, g_scales, w2, d, ga
             T["dh", e, h] = (codes, scales)
 
         def stage_2(e, u):
-            o = work.tile([P, PACK, F], F32, name="o", tag="o", bufs=3)
+            o = work.tile([P, PACK, F], F32, name="o", tag="o", bufs=4)
             T["o", e, u] = o
             for j in range(PACK):
                 acc = psum.tile([P, F], F32, name="acc", tag="acc")
@@ -249,11 +253,11 @@ def tile_expert_inner_weight_gradient_e3_kernel(tc, g_words, g_scales, w2, d, ga
                 load_w(e + 2, 1)
                 load_g(e + 2)
                 load_x(e + 2, 0)
+                load_d(e + 2)
+                load_x(e + 2, 1)
                 if e > 0:
                     store(e - 1, 0)
                     store(e - 1, 1)
-                load_d(e + 2)
-                load_x(e + 2, 1)
                 load_m(e + 2)
             elif e > 0:
                 store(e - 1, 0)

@@ -21,7 +21,7 @@ PACK = 4
 K_PASS = P * PACK
 HALVES = C // K_PASS
 
-VECTOR_COPIES = {("w", 0, 1), ("x", 0, 0, 1), ("x", 1, 1, 1), ("dh", 3, 1)}
+VECTOR_COPIES = {("w", 0, 1), ("dh", 3, 1)}
 GPSIMD_W = (1, 2, 3)
 
 
@@ -92,8 +92,8 @@ def tile_expert_inner_weight_gradient_e3_kernel(tc, g_words, g_scales, w2, d, ga
         def permute_g(e):
             codes = work.tile([P, 2, C], I32, name="g_codes", tag="g_codes", bufs=2, align_bytes=64)
             nc.vector.tensor_copy(
-                out=codes[:].rearrange("p g (h t m) -> p (g h) m t", h=HALVES, t=PACK),
-                in_=T["g_raw", e][:].rearrange("p g (h m t) -> p (g h) m t", h=HALVES, t=PACK),
+                out=codes[:].rearrange("p g (h t b i) -> p (g h) b t i", h=HALVES, t=PACK, i=4),
+                in_=T["g_raw", e][:].rearrange("p g (h b i t) -> p (g h) b t i", h=HALVES, t=PACK, i=4),
             )
             T["g_codes", e] = codes
 
@@ -101,8 +101,8 @@ def tile_expert_inner_weight_gradient_e3_kernel(tc, g_words, g_scales, w2, d, ga
             scales = work.tile([P, 2, C], U8, name="g_scale", tag="g_scale", bufs=2, align_bytes=64)
             for g in range(2):
                 nc.vector.tensor_copy(
-                    out=scales[:, g, :].rearrange("p (h t m) -> p h m t", h=HALVES, t=PACK),
-                    in_=gs_raw[:, g, C * e:C * (e + 1)].rearrange("p (h m t) -> p h m t", h=HALVES, t=PACK),
+                    out=scales[:, g, :].rearrange("p (h t b i) -> p h b t i", h=HALVES, t=PACK, i=16),
+                    in_=gs_raw[:, g, C * e:C * (e + 1)].rearrange("p (h b i t) -> p h b t i", h=HALVES, t=PACK, i=16),
                 )
             T["g_scale", e] = scales
 

@@ -1,6 +1,7 @@
 from contextlib import ExitStack
 
 import concourse.mybir as mybir
+from concourse.masks import make_identity
 
 E, C, D, F = 4, 1024, 1024, 512
 BETA = 0.9
@@ -21,7 +22,7 @@ PACK = 4
 K_PASS = P * PACK
 HALVES = C // K_PASS
 
-VECTOR_COPIES = {("w", 0, 1), ("dh", 3, 1)}
+VECTOR_COPIES = {("w", 0, 1)}
 GPSIMD_W = (1, 2, 3)
 
 
@@ -34,6 +35,7 @@ def tile_expert_inner_weight_gradient_e3_kernel(tc, g_words, g_scales, w2, d, ga
         keep = ctx.enter_context(tc.tile_pool(name="keep", bufs=1))
         psum = ctx.enter_context(tc.psum_pool(name="psum", bufs=8))
 
+        ctx.enter_context(tc.manual_schedule())
         T = {}
 
         def load_w(e, g):
@@ -98,7 +100,7 @@ def tile_expert_inner_weight_gradient_e3_kernel(tc, g_words, g_scales, w2, d, ga
             T["g_codes", e] = codes
 
         def permute_gs(e):
-            scales = work.tile([P, 2, C], U8, name="g_scale", tag="g_scale", bufs=2, align_bytes=64)
+            scales = work.tile([P, 2, C], U8, name="g_scale", tag="g_scale", bufs=4, align_bytes=64)
             for g in range(2):
                 nc.vector.tensor_copy(
                     out=scales[:, g, :].rearrange("p (h t b i) -> p h b t i", h=HALVES, t=PACK, i=16),
@@ -123,13 +125,16 @@ def tile_expert_inner_weight_gradient_e3_kernel(tc, g_words, g_scales, w2, d, ga
 
         def stage_1(e, h):
             dh = work.tile([P, PACK, F], BF16, name="dh_lin", tag="dh_lin", bufs=2, align_bytes=64)
+            accs = []
             for t in range(PACK):
                 acc = psum.tile([P, F], F32, name="acc", tag="acc")
-                cols = slice((PACK * h + t) * P, (PACK * h + t + 1) * P)
-                for g in range(2):
-                    codes, scales = T["w", e, g]
+                accs.append(acc)
+            for g in range(2):
+                codes, scales = T["w", e, g]
+                for t in range(PACK):
+                    cols = slice((PACK * h + t) * P, (PACK * h + t + 1) * P)
                     nc.tensor.matmul_mx(
-                        out=acc[:],
+                        out=accs[t][:],
                         lhsT=T["g_codes", e][:, g, cols].bitcast(E5M2),
                         lhsT_scale=T["g_scale", e][:, g, cols],
                         rhs=codes[:].bitcast(E4M3),
@@ -137,8 +142,14 @@ def tile_expert_inner_weight_gradient_e3_kernel(tc, g_words, g_scales, w2, d, ga
                         start=(g == 0),
                         stop=(g == 1),
                     )
+            for t in range(PACK):
                 nc.vector.scalar_tensor_tensor(
-                    out=dh[:, t, :], in0=acc[:], scalar=gate_sb[:, HALVES * e + h, t:t + 1], in1=T["d_raw", e][:, h, t, :], op0=MULT, op1=MULT
+                    out=dh[:, t, :],
+                    in0=accs[t][:],
+                    scalar=gate_sb[:, t, HALVES * e + h:HALVES * e + h + 1],
+                    in1=T["d_raw", e][:, h, t, :],
+                    op0=MULT,
+                    op1=MULT,
                 )
             T["dh_lin", e, h] = dh
 
@@ -157,17 +168,20 @@ def tile_expert_inner_weight_gradient_e3_kernel(tc, g_words, g_scales, w2, d, ga
             nc.vector.quantize_mx(out=codes[:].bitcast(E5M2), scales=scales[:], in_=T["dh_grp", e, h][:].rearrange("p c t -> p (c t)"))
             T["dh", e, h] = (codes, scales)
 
-        def stage_2(e, u):
-            o = work.tile([P, PACK, F], F32, name="o", tag="o", bufs=4)
+        def stage_2(e, u, before_last_two=None):
+            o = work.tile([P, PACK, F], F32, name="o", tag="o", bufs=4, align_bytes=64)
             T["o", e, u] = o
+            accs = []
             for j in range(PACK):
                 acc = psum.tile([P, F], F32, name="acc", tag="acc")
-                cols = slice((PACK * u + j) * P, (PACK * u + j + 1) * P)
-                for h in range(HALVES):
-                    xc, xs = T["x", e, h]
-                    hc, hs = T["dh", e, h]
+                accs.append(acc)
+            for h in range(HALVES):
+                xc, xs = T["x", e, h]
+                hc, hs = T["dh", e, h]
+                for j in range(PACK):
+                    cols = slice((PACK * u + j) * P, (PACK * u + j + 1) * P)
                     nc.tensor.matmul_mx(
-                        out=acc[:],
+                        out=accs[j][:],
                         lhsT=xc[:, cols].bitcast(E4M3),
                         lhsT_scale=xs[:, cols],
                         rhs=hc[:].bitcast(E5M2),
@@ -175,79 +189,88 @@ def tile_expert_inner_weight_gradient_e3_kernel(tc, g_words, g_scales, w2, d, ga
                         start=(h == 0),
                         stop=(h == HALVES - 1),
                     )
-                nc.vector.scalar_tensor_tensor(out=o[:, j, :], in0=T["m_raw", e][:, PACK * u + j, :], scalar=BETA, in1=acc[:], op0=MULT, op1=ADD)
-                if e == E - 1 and (j % 2 == 1 or u == 1):
-                    j0 = j if u == 1 else j - 1
-                    store(e, u, j0, j + 1)
+            for j in range(PACK):
+                if j == 2 and before_last_two:
+                    before_last_two()
+                nc.vector.scalar_tensor_tensor(out=o[:, j, :], in0=T["m_raw", e][:, PACK * u + j, :], scalar=BETA, in1=accs[j][:], op0=MULT, op1=ADD)
+                if (e, u) == (E - 1, 1) and j >= 2:
+                    store(e, u, j, j + 1)
+                elif e >= E - 2 and j % 2 == 1:
+                    store(e, u, j - 1, j + 1)
 
         def store(e, u, j0=0, j1=PACK):
             nc.sync.dma_start(out=out[e].rearrange("(p r) f -> p r f", r=8)[:, PACK * u + j0:PACK * u + j1, :], in_=T["o", e, u][:, j0:j1, :])
 
-        gs_raw = keep.tile([P, 2, E * C], U8, name="gs_raw", align_bytes=64)
+        gs_raw = work.tile([P, 2, E * C], U8, name="gs_raw", tag="o", bufs=4, align_bytes=64)
         nc.vector.memset(gs_raw[:].rearrange("p g n -> p (g n)").bitcast(I32), 0)
-        gate_sb = keep.tile([P, E * HALVES, PACK], BF16, name="gate_sb")
-        nc.scalar.dma_start(out=gate_sb[:], in_=gate.rearrange("e c -> (e c)").rearrange("(u p t) -> p u t", p=P, t=PACK))
+        gate_rows = keep.tile([P, PACK * P], BF16, name="gate_rows")
+        nc.gpsimd.memset(gate_rows[:], 0.0)
+        identity = keep.tile([P, P], BF16, name="identity")
+        make_identity(nc, identity[:])
         load_w(0, 0)
         load_w(0, 1)
         for q in range(4):
-            nc.scalar.dma_start(
+            nc.sync.dma_start(
                 out=gs_raw[32 * q:32 * q + 4, :, :].bitcast(I32),
                 in_=g_scales[:, 4 * q:4 * q + 4, :].rearrange("g q n -> q g n").bitcast(I32),
             )
-        load_x(0, 0)
+        nc.sync.dma_start(out=gate_rows[0:E * HALVES, :], in_=gate.rearrange("e (h c) -> (e h) c", h=HALVES))
         load_g(0)
-        load_x(0, 1)
+        load_x(0, 0)
         load_d(0)
+        load_x(0, 1)
         load_w(1, 0)
         load_w(1, 1)
         load_g(1)
         load_x(1, 0)
         load_d(1)
-        load_m(0)
         load_x(1, 1)
-        load_m(1)
+        load_m(0)
 
         interleave_w(0, 0)
         interleave_w(0, 1)
         interleave_x(0, 0, 0)
-        quantize_w(0, 0)
-        permute_g(0)
-        quantize_w(0, 1)
-        permute_gs(0)
         interleave_x(0, 0, 1)
+        gate_psum = psum.tile([P, PACK, P], BF16, name="gate_psum", tag="acc")
+        for t in range(PACK):
+            nc.tensor.transpose(gate_psum[:, t, :], gate_rows[:].rearrange("r (m t) -> r t m", t=PACK)[:, t, :], identity[:])
+        gate_sb = keep.tile([P, PACK, E * HALVES], F32, name="gate_sb")
+        nc.vector.tensor_copy(out=gate_sb[:], in_=gate_psum[:, :, 0:E * HALVES])
+        permute_g(0)
+        permute_gs(0)
+        quantize_w(0, 1)
+        quantize_w(0, 0)
+        permute_gs(1)
 
         for e in range(E):
             more = e + 1 < E
-            if not more:
-                interleave_x(e, 1, 0)
-            stage_1(e, 0)
-            interleave_dh(e, 0)
             if more:
                 interleave_w(e + 1, 0)
-            else:
-                interleave_x(e, 1, 1)
+                interleave_w(e + 1, 1)
+            interleave_x(e, 1, 0)
+            stage_1(e, 0)
+            interleave_dh(e, 0)
             quantize_x(e, 0)
             stage_1(e, 1)
+            interleave_x(e, 1, 1)
             interleave_dh(e, 1)
-            if more:
-                interleave_w(e + 1, 1)
-            quantize_dh(e, 0)
             if e > 0:
                 stage_2(e - 1, 0)
-            quantize_dh(e, 1)
+            else:
+                permute_gs(2)
+                permute_gs(3)
+            quantize_dh(e, 0)
+            quantize_x(e, 1)
             if more:
-                permute_gs(e + 1)
                 permute_g(e + 1)
                 quantize_w(e + 1, 0)
-                interleave_x(e, 1, 0)
-                interleave_x(e, 1, 1)
-            if e > 0:
-                stage_2(e - 1, 1)
-            if more:
                 quantize_w(e + 1, 1)
                 interleave_x(e + 1, 0, 0)
                 interleave_x(e + 1, 0, 1)
-            quantize_x(e, 1)
+            if e > 0:
+                stage_2(e - 1, 1, before_last_two=lambda: quantize_dh(e, 1))
+            else:
+                quantize_dh(e, 1)
             if e + 2 < E:
                 load_w(e + 2, 0)
                 load_w(e + 2, 1)
@@ -255,12 +278,10 @@ def tile_expert_inner_weight_gradient_e3_kernel(tc, g_words, g_scales, w2, d, ga
                 load_x(e + 2, 0)
                 load_d(e + 2)
                 load_x(e + 2, 1)
-                if e > 0:
-                    store(e - 1, 0)
-                    store(e - 1, 1)
-                load_m(e + 2)
-            elif e > 0:
+            if 0 < e < E - 1:
                 store(e - 1, 0)
                 store(e - 1, 1)
+            if more:
+                load_m(e + 1)
         stage_2(E - 1, 0)
         stage_2(E - 1, 1)

@@ -22,7 +22,7 @@ PACK = 4
 K_PASS = P * PACK
 HALVES = C // K_PASS
 
-VECTOR_COPIES = {("w", 0, 1)}
+VECTOR_COPIES = {("w", 0, 1), ("x", 0, 1, 1)}
 GPSIMD_W = (1, 2, 3)
 
 
@@ -129,10 +129,10 @@ def tile_expert_inner_weight_gradient_e3_kernel(tc, g_words, g_scales, w2, d, ga
             for t in range(PACK):
                 acc = psum.tile([P, F], F32, name="acc", tag="acc")
                 accs.append(acc)
-            for g in range(2):
-                codes, scales = T["w", e, g]
-                for t in range(PACK):
-                    cols = slice((PACK * h + t) * P, (PACK * h + t + 1) * P)
+            for t in range(PACK):
+                cols = slice((PACK * h + t) * P, (PACK * h + t + 1) * P)
+                for g in range(2):
+                    codes, scales = T["w", e, g]
                     nc.tensor.matmul_mx(
                         out=accs[t][:],
                         lhsT=T["g_codes", e][:, g, cols].bitcast(E5M2),
@@ -214,13 +214,13 @@ def tile_expert_inner_weight_gradient_e3_kernel(tc, g_words, g_scales, w2, d, ga
                 out=gs_raw[32 * q:32 * q + 4, :, :].bitcast(I32),
                 in_=g_scales[:, 4 * q:4 * q + 4, :].rearrange("g q n -> q g n").bitcast(I32),
             )
+        load_x(0, 0)
         nc.sync.dma_start(out=gate_rows[0:E * HALVES, :], in_=gate.rearrange("e (h c) -> (e h) c", h=HALVES))
         load_g(0)
-        load_x(0, 0)
         load_d(0)
-        load_x(0, 1)
         load_w(1, 0)
         load_w(1, 1)
+        load_x(0, 1)
         load_g(1)
         load_x(1, 0)
         load_d(1)
@@ -231,34 +231,38 @@ def tile_expert_inner_weight_gradient_e3_kernel(tc, g_words, g_scales, w2, d, ga
         interleave_w(0, 1)
         interleave_x(0, 0, 0)
         interleave_x(0, 0, 1)
+        permute_gs(0)
+        permute_gs(1)
         gate_psum = psum.tile([P, PACK, P], BF16, name="gate_psum", tag="acc")
         for t in range(PACK):
             nc.tensor.transpose(gate_psum[:, t, :], gate_rows[:].rearrange("r (m t) -> r t m", t=PACK)[:, t, :], identity[:])
         gate_sb = keep.tile([P, PACK, E * HALVES], F32, name="gate_sb")
         nc.vector.tensor_copy(out=gate_sb[:], in_=gate_psum[:, :, 0:E * HALVES])
-        permute_g(0)
-        permute_gs(0)
+        permute_gs(2)
         quantize_w(0, 1)
         quantize_w(0, 0)
-        permute_gs(1)
+        permute_g(0)
+        permute_gs(3)
 
         for e in range(E):
             more = e + 1 < E
             if more:
                 interleave_w(e + 1, 0)
                 interleave_w(e + 1, 1)
-            interleave_x(e, 1, 0)
+            if e > 0:
+                interleave_x(e, 1, 0)
             stage_1(e, 0)
             interleave_dh(e, 0)
-            quantize_x(e, 0)
+            if e == 0:
+                interleave_x(e, 1, 0)
             stage_1(e, 1)
-            interleave_x(e, 1, 1)
-            interleave_dh(e, 1)
             if e > 0:
+                interleave_x(e, 1, 1)
                 stage_2(e - 1, 0)
-            else:
-                permute_gs(2)
-                permute_gs(3)
+            quantize_x(e, 0)
+            if e == 0:
+                interleave_x(e, 1, 1)
+            interleave_dh(e, 1)
             quantize_dh(e, 0)
             quantize_x(e, 1)
             if more:

from contextlib import ExitStack

import concourse.mybir as mybir
from concourse.masks import make_identity

E, C, D, F = 4, 1024, 1024, 512
BETA = 0.9
FLOPS = 2 * (2 * E * C * D * F)

F32 = mybir.dt.float32
BF16 = mybir.dt.bfloat16
I32 = mybir.dt.int32
U32 = mybir.dt.uint32
U8 = mybir.dt.uint8
E4M3 = mybir.dt.float8_e4m3fn_x4
E5M2 = mybir.dt.float8_e5m2_x4
MULT = mybir.AluOpType.mult
ADD = mybir.AluOpType.add

P = 128
PACK = 4
K_PASS = P * PACK
HALVES = C // K_PASS

VECTOR_COPIES = {("w", 0, 1), ("x", 0, 1, 1)}
GPSIMD_W = (1, 2, 3)


def tile_expert_inner_weight_gradient_e3_kernel(tc, g_words, g_scales, w2, d, gate, x, m, out):
    nc = tc.nc

    with ExitStack() as ctx:
        raw = ctx.enter_context(tc.tile_pool(name="raw", bufs=2))
        work = ctx.enter_context(tc.tile_pool(name="work", bufs=2))
        keep = ctx.enter_context(tc.tile_pool(name="keep", bufs=1))
        psum = ctx.enter_context(tc.psum_pool(name="psum", bufs=8))

        ctx.enter_context(tc.manual_schedule())
        T = {}

        def load_w(e, g):
            t = raw.tile([P, PACK, F], BF16, name="w_raw", tag="w_raw", bufs=4)
            nc.sync.dma_start(out=t[:], in_=w2[e, g * K_PASS:(g + 1) * K_PASS, :].rearrange("(p t) f -> p t f", t=PACK))
            T["w_raw", e, g] = t

        def load_g(e):
            t = raw.tile([P, 2, C], I32, name="g_raw", tag="g_raw", bufs=2)
            src = g_words.rearrange("g p n t -> p g (n t)")[:, :, 4 * C * e:4 * C * (e + 1)].bitcast(I32)
            nc.sync.dma_start(out=t[:], in_=src)
            T["g_raw", e] = t

        def load_d(e):
            t = raw.tile([P, HALVES, PACK, F], BF16, name="d_raw", tag="d_raw", bufs=2)
            nc.sync.dma_start(out=t[:].rearrange("p h t f -> p h (t f)"), in_=d[e].rearrange("(h p t) f -> p h (t f)", h=HALVES, t=PACK))
            T["d_raw", e] = t

        def load_x(e, h):
            t = raw.tile([P, PACK, D], BF16, name="x_raw", tag="x_raw", bufs=4)
            nc.sync.dma_start(out=t[:], in_=x[e, h * K_PASS:(h + 1) * K_PASS, :].rearrange("(p t) f -> p t f", t=PACK))
            T["x_raw", e, h] = t

        def load_m(e):
            t = raw.tile([P, 8, F], BF16, name="m_raw", tag="m_raw", bufs=2)
            nc.sync.dma_start(out=t[:], in_=m[e].rearrange("(p r) f -> p r f", r=8))
            T["m_raw", e] = t

        def interleaving_copy(key, out, in_):
            if key in VECTOR_COPIES:
                nc.vector.tensor_copy(out=out, in_=in_)
            else:
                nc.scalar.copy(out=out, in_=in_)

        def interleave_w(e, g):
            t = work.tile([P, F, PACK], BF16, name="w_grp", tag="w_grp", bufs=2, align_bytes=64)
            if e in GPSIMD_W:
                for c in range(0, F, P):
                    nc.gpsimd.tensor_scalar(
                        out=t[:, c:c + P, :], in0=T["w_raw", e, g][:, :, c:c + P].rearrange("p t c -> p c t"), scalar1=1.0, scalar2=0.0, op0=MULT, op1=ADD
                    )
            else:
                interleaving_copy(
                    ("w", e, g),
                    out=t[:].rearrange("p (c i) t -> p c t i", i=4),
                    in_=T["w_raw", e, g][:].rearrange("p t (c i) -> p c t i", i=4),
                )
            T["w_grp", e, g] = t

        def quantize_w(e, g):
            codes = work.tile([P, F], U32, name="w_codes", tag="w_codes", bufs=4, align_bytes=64)
            scales = work.tile([P, F], U8, name="w_scales", tag="w_scales", bufs=4, align_bytes=64)
            nc.vector.quantize_mx(out=codes[:].bitcast(E4M3), scales=scales[:], in_=T["w_grp", e, g][:].rearrange("p c t -> p (c t)"))
            T["w", e, g] = (codes, scales)

        def permute_g(e):
            codes = work.tile([P, 2, C], I32, name="g_codes", tag="g_codes", bufs=2, align_bytes=64)
            nc.vector.tensor_copy(
                out=codes[:].rearrange("p g (h t b i) -> p (g h) b t i", h=HALVES, t=PACK, i=4),
                in_=T["g_raw", e][:].rearrange("p g (h b i t) -> p (g h) b t i", h=HALVES, t=PACK, i=4),
            )
            T["g_codes", e] = codes

        def permute_gs(e):
            scales = work.tile([P, 2, C], U8, name="g_scale", tag="g_scale", bufs=4, align_bytes=64)
            for g in range(2):
                nc.vector.tensor_copy(
                    out=scales[:, g, :].rearrange("p (h t b i) -> p h b t i", h=HALVES, t=PACK, i=16),
                    in_=gs_raw[:, g, C * e:C * (e + 1)].rearrange("p (h b i t) -> p h b t i", h=HALVES, t=PACK, i=16),
                )
            T["g_scale", e] = scales

        def interleave_x(e, h, u):
            if ("x_grp", e, h) not in T:
                T["x_grp", e, h] = work.tile([P, D, PACK], BF16, name="x_grp", tag="x_grp", bufs=2, align_bytes=64)
            interleaving_copy(
                ("x", e, h, u),
                out=T["x_grp", e, h][:].rearrange("p (u j m) t -> p u m t j", u=2, j=4)[:, u],
                in_=T["x_raw", e, h][:].rearrange("p t (m u j) -> p u m t j", u=2, j=4)[:, u],
            )

        def quantize_x(e, h):
            codes = work.tile([P, D], U32, name="x_codes", tag="x_codes", bufs=4, align_bytes=64)
            scales = work.tile([P, D], U8, name="x_scales", tag="x_scales", bufs=4, align_bytes=64)
            nc.vector.quantize_mx(out=codes[:].bitcast(E4M3), scales=scales[:], in_=T["x_grp", e, h][:].rearrange("p c t -> p (c t)"))
            T["x", e, h] = (codes, scales)

        def stage_1(e, h):
            dh = work.tile([P, PACK, F], BF16, name="dh_lin", tag="dh_lin", bufs=2, align_bytes=64)
            accs = []
            for t in range(PACK):
                acc = psum.tile([P, F], F32, name="acc", tag="acc")
                accs.append(acc)
            for t in range(PACK):
                cols = slice((PACK * h + t) * P, (PACK * h + t + 1) * P)
                for g in range(2):
                    codes, scales = T["w", e, g]
                    nc.tensor.matmul_mx(
                        out=accs[t][:],
                        lhsT=T["g_codes", e][:, g, cols].bitcast(E5M2),
                        lhsT_scale=T["g_scale", e][:, g, cols],
                        rhs=codes[:].bitcast(E4M3),
                        rhs_scale=scales[:],
                        start=(g == 0),
                        stop=(g == 1),
                    )
            for t in range(PACK):
                nc.vector.scalar_tensor_tensor(
                    out=dh[:, t, :],
                    in0=accs[t][:],
                    scalar=gate_sb[:, t, HALVES * e + h:HALVES * e + h + 1],
                    in1=T["d_raw", e][:, h, t, :],
                    op0=MULT,
                    op1=MULT,
                )
            T["dh_lin", e, h] = dh

        def interleave_dh(e, h):
            t = work.tile([P, F, PACK], BF16, name="dh_grp", tag="dh_grp", bufs=2, align_bytes=64)
            interleaving_copy(
                ("dh", e, h),
                out=t[:].rearrange("p (c i) t -> p c t i", i=4),
                in_=T["dh_lin", e, h][:].rearrange("p t (c i) -> p c t i", i=4),
            )
            T["dh_grp", e, h] = t

        def quantize_dh(e, h):
            codes = work.tile([P, F], U32, name="dh_codes", tag="dh_codes", bufs=4, align_bytes=64)
            scales = work.tile([P, F], U8, name="dh_scales", tag="dh_scales", bufs=4, align_bytes=64)
            nc.vector.quantize_mx(out=codes[:].bitcast(E5M2), scales=scales[:], in_=T["dh_grp", e, h][:].rearrange("p c t -> p (c t)"))
            T["dh", e, h] = (codes, scales)

        def stage_2(e, u, before_last_two=None):
            o = work.tile([P, PACK, F], F32, name="o", tag="o", bufs=4, align_bytes=64)
            T["o", e, u] = o
            accs = []
            for j in range(PACK):
                acc = psum.tile([P, F], F32, name="acc", tag="acc")
                accs.append(acc)
            for h in range(HALVES):
                xc, xs = T["x", e, h]
                hc, hs = T["dh", e, h]
                for j in range(PACK):
                    cols = slice((PACK * u + j) * P, (PACK * u + j + 1) * P)
                    nc.tensor.matmul_mx(
                        out=accs[j][:],
                        lhsT=xc[:, cols].bitcast(E4M3),
                        lhsT_scale=xs[:, cols],
                        rhs=hc[:].bitcast(E5M2),
                        rhs_scale=hs[:],
                        start=(h == 0),
                        stop=(h == HALVES - 1),
                    )
            for j in range(PACK):
                if j == 2 and before_last_two:
                    before_last_two()
                nc.vector.scalar_tensor_tensor(out=o[:, j, :], in0=T["m_raw", e][:, PACK * u + j, :], scalar=BETA, in1=accs[j][:], op0=MULT, op1=ADD)
                if (e, u) == (E - 1, 1) and j >= 2:
                    store(e, u, j, j + 1)
                elif e >= E - 2 and j % 2 == 1:
                    store(e, u, j - 1, j + 1)

        def store(e, u, j0=0, j1=PACK):
            nc.sync.dma_start(out=out[e].rearrange("(p r) f -> p r f", r=8)[:, PACK * u + j0:PACK * u + j1, :], in_=T["o", e, u][:, j0:j1, :])

        gs_raw = work.tile([P, 2, E * C], U8, name="gs_raw", tag="o", bufs=4, align_bytes=64)
        nc.vector.memset(gs_raw[:].rearrange("p g n -> p (g n)").bitcast(I32), 0)
        gate_rows = keep.tile([P, PACK * P], BF16, name="gate_rows")
        nc.gpsimd.memset(gate_rows[:], 0.0)
        identity = keep.tile([P, P], BF16, name="identity")
        make_identity(nc, identity[:])
        load_w(0, 0)
        load_w(0, 1)
        for q in range(4):
            nc.sync.dma_start(
                out=gs_raw[32 * q:32 * q + 4, :, :].bitcast(I32),
                in_=g_scales[:, 4 * q:4 * q + 4, :].rearrange("g q n -> q g n").bitcast(I32),
            )
        load_x(0, 0)
        nc.sync.dma_start(out=gate_rows[0:E * HALVES, :], in_=gate.rearrange("e (h c) -> (e h) c", h=HALVES))
        load_g(0)
        load_d(0)
        load_w(1, 0)
        load_w(1, 1)
        load_x(0, 1)
        load_g(1)
        load_x(1, 0)
        load_d(1)
        load_x(1, 1)
        load_m(0)

        interleave_w(0, 0)
        interleave_w(0, 1)
        interleave_x(0, 0, 0)
        interleave_x(0, 0, 1)
        permute_gs(0)
        permute_gs(1)
        gate_psum = psum.tile([P, PACK, P], BF16, name="gate_psum", tag="acc")
        for t in range(PACK):
            nc.tensor.transpose(gate_psum[:, t, :], gate_rows[:].rearrange("r (m t) -> r t m", t=PACK)[:, t, :], identity[:])
        gate_sb = keep.tile([P, PACK, E * HALVES], F32, name="gate_sb")
        nc.vector.tensor_copy(out=gate_sb[:], in_=gate_psum[:, :, 0:E * HALVES])
        permute_gs(2)
        quantize_w(0, 1)
        quantize_w(0, 0)
        permute_g(0)
        permute_gs(3)

        for e in range(E):
            more = e + 1 < E
            if more:
                interleave_w(e + 1, 0)
                interleave_w(e + 1, 1)
            if e > 0:
                interleave_x(e, 1, 0)
            stage_1(e, 0)
            interleave_dh(e, 0)
            if e == 0:
                interleave_x(e, 1, 0)
            stage_1(e, 1)
            if e > 0:
                interleave_x(e, 1, 1)
                stage_2(e - 1, 0)
            quantize_x(e, 0)
            if e == 0:
                interleave_x(e, 1, 1)
            interleave_dh(e, 1)
            quantize_dh(e, 0)
            quantize_x(e, 1)
            if more:
                permute_g(e + 1)
                quantize_w(e + 1, 0)
                quantize_w(e + 1, 1)
                interleave_x(e + 1, 0, 0)
                interleave_x(e + 1, 0, 1)
            if e > 0:
                stage_2(e - 1, 1, before_last_two=lambda: quantize_dh(e, 1))
            else:
                quantize_dh(e, 1)
            if e + 2 < E:
                load_w(e + 2, 0)
                load_w(e + 2, 1)
                load_g(e + 2)
                load_x(e + 2, 0)
                load_d(e + 2)
                load_x(e + 2, 1)
            if 0 < e < E - 1:
                store(e - 1, 0)
                store(e - 1, 1)
            if more:
                load_m(e + 1)
        stage_2(E - 1, 0)
        stage_2(E - 1, 1)
